import numpy as np, ml_dtypes
CORES = [18,19,22,23,26,27,30,31,98,99,102,103,106,107,110,111]
N = 16
GROUPS = [[0,1,2,3],[4,5,6,7],[8,9,10,11],[12,13,14,15]]
def setup_inputs(rng):
    return {"x": rng.standard_normal((N, 128, 2048), dtype=np.float32).astype(ml_dtypes.bfloat16)}
def reference(x):
    y = np.empty((N, 128, 512), x.dtype)
    for g in GROUPS:
        s = x[g].sum(axis=0, dtype=np.float64).astype(x[g].dtype)
        n = len(g); b = x.shape[2] // n
        for i, r in enumerate(g):
            y[r] = s[:, i * b:(i + 1) * b]
    return {"y": y}

@@ -1,0 +1,58 @@
+from concourse.bass import DstId, RemoteDMATransfer
+from concourse.mybir import AluOpType
+
+B = 512
+
+SCRATCH = {
+    "xs": ("dram", [3, 128, B], "bfloat16"),
+    "land": ("dram", [2, 128, B], "bfloat16"),
+    "fl": ("dram", [128, B], "bfloat16"),
+}
+SEMAPHORES = ["ldA", "ldB", "ldD", "own", "go", "sent", "arr", "fsent", "farr", "done"]
+
+ALL16 = 0xFFFF
+
+
+def rank_program(g, core, T, topo):
+    rank = T.rank_of(core)
+    if rank is None:
+        return
+    grp = [gr for gr in T.tables["GROUPS"] if rank in gr][0]
+    i = grp.index(rank)
+    S = T.sem
+
+    def peer(k):
+        return T.cores[grp[k]]
+
+    def cols(b):
+        return T.x[:, b * B:(b + 1) * B]
+
+    g.sync.dma_start(T.xs[0], cols(i ^ 1)).then_inc(S.ldA, 16)
+    g.scalar.dma_start(T.xs[1], cols(i ^ 3)).then_inc(S.ldB, 16)
+    g.sync.dma_start(T.xs[2], cols(i ^ 2)).then_inc(S.ldD, 16)
+
+    rid, pid, _ = topo.addr(peer(i ^ 3))
+    g.wait_ge(S.ldA, 16)
+    g.remote_dma(T.land[1], T.xs[0], S.arr, S.sent, pid, rid, ALL16)
+    rid, pid, _ = topo.addr(peer(i ^ 1))
+    g.wait_ge(S.ldB, 16)
+    g.remote_dma(T.land[0], T.xs[1], S.arr, S.sent, pid, rid, ALL16)
+    g.sem_inc(S.go, 1)
+
+    g.scalar.wait_ge(S.go, 1)
+    g.scalar.dma_start(T.y[:], cols(i)).then_inc(S.own, 16)
+
+    rid, pid, _ = topo.addr(peer(i ^ 2))
+    g.wait_ge(S.ldD, 16)
+    g.wait_ge(S.arr, 32)
+    g.remote_dma_fused(
+        [RemoteDMATransfer(dst_ids=[DstId(rid=rid, pnc=pid)], dma_engine_mask=ALL16, remote_sem=S.farr,
+                           srcs=[T.xs[2], T.land[0], T.land[1]], dsts=[T.fl[:]], alu_op=1)],
+        local_sem=S.fsent)
+
+    g.wait_ge(S.own, 16)
+    g.wait_ge(S.farr, 16)
+    g.dma_start(T.y[:], T.fl[:], accum_op=AluOpType.add, max_dma_last_dim=4096).then_inc(S.done, 16)
+    g.wait_ge(S.sent, 32)
+    g.wait_ge(S.fsent, 16)
+    g.wait_ge(S.done, 16)

@@ -2,24 +2,44 @@ from concourse.bass import DstId, RemoteDMATransfer
 from concourse.mybir import AluOpType
 
 B = 512
+H = 256
 
 SCRATCH = {
-    "xs": ("dram", [3, 128, B], "bfloat16"),
-    "land": ("dram", [2, 128, B], "bfloat16"),
-    "fl": ("dram", [128, B], "bfloat16"),
+    "xs": ("dram", [6, 128, H], "bfloat16"),
+    "land": ("dram", [3, 128, H], "bfloat16"),
+    "fl": ("dram", [2, 128, H], "bfloat16"),
 }
 SEMAPHORES = ["ldA", "ldB", "ldD", "own", "go", "sent", "arr", "fsent", "farr", "done"]
 
 ALL16 = 0xFFFF
+LO8 = 0x00FF
+HI8 = 0xFF00
 
 
 def rank_program(g, core, T, topo):
+    S = T.sem
+
+    def dst(c):
+        rid, pid, _ = topo.addr(c)
+        return DstId(rid=rid, pnc=pid)
+
+    def fold(srcs, owner, h):
+        g.remote_dma_fused(
+            [RemoteDMATransfer(dst_ids=[dst(owner)], dma_engine_mask=ALL16, remote_sem=S.farr,
+                               srcs=srcs, dsts=[T.fl[h]], alu_op=1)],
+            local_sem=S.fsent)
+
     rank = T.rank_of(core)
     if rank is None:
+        if core + 2 >= 112 or topo.chip(core + 2) != topo.chip(core) or T.rank_of(core + 2) is None:
+            return
+        g.wait_ge(S.arr, 32)
+        fold([T.land[0], T.land[1], T.land[2]], core + 2, 1)
+        g.wait_ge(S.fsent, 16)
         return
+
     grp = [gr for gr in T.tables["GROUPS"] if rank in gr][0]
     i = grp.index(rank)
-    S = T.sem
 
     def peer(k):
         return T.cores[grp[k]]
@@ -27,32 +47,36 @@ def rank_program(g, core, T, topo):
     def cols(b):
         return T.x[:, b * B:(b + 1) * B]
 
-    g.sync.dma_start(T.xs[0], cols(i ^ 1)).then_inc(S.ldA, 16)
-    g.scalar.dma_start(T.xs[1], cols(i ^ 3)).then_inc(S.ldB, 16)
-    g.sync.dma_start(T.xs[2], cols(i ^ 2)).then_inc(S.ldD, 16)
+    g.sync.dma_start(T.xs[0:2], cols(i ^ 1)).then_inc(S.ldA, 16)
+    g.scalar.dma_start(T.xs[2:4], cols(i ^ 3)).then_inc(S.ldB, 16)
+    g.sync.dma_start(T.xs[4:6], cols(i ^ 2)).then_inc(S.ldD, 16)
 
-    rid, pid, _ = topo.addr(peer(i ^ 3))
+    def send(slot, k, mslot):
+        g.remote_dma_fused(
+            [RemoteDMATransfer(dst_ids=[dst(peer(i ^ k ^ 2))], dma_engine_mask=LO8, remote_sem=S.arr,
+                               src=T.xs[slot], dst=T.land[mslot]),
+             RemoteDMATransfer(dst_ids=[dst(peer(i ^ k) - 2)], dma_engine_mask=HI8, remote_sem=S.arr,
+                               src=T.xs[slot + 1], dst=T.land[k - 1])],
+            local_sem=S.sent)
+
     g.wait_ge(S.ldA, 16)
-    g.remote_dma(T.land[1], T.xs[0], S.arr, S.sent, pid, rid, ALL16)
-    rid, pid, _ = topo.addr(peer(i ^ 1))
+    send(0, 1, 1)
     g.wait_ge(S.ldB, 16)
-    g.remote_dma(T.land[0], T.xs[1], S.arr, S.sent, pid, rid, ALL16)
+    send(2, 3, 0)
+    g.wait_ge(S.ldD, 16)
+    rid, pid, _ = topo.addr(peer(i ^ 2) - 2)
+    g.remote_dma(T.land[1], T.xs[5], S.arr, S.sent, pid, rid, ALL16)
     g.sem_inc(S.go, 1)
 
     g.scalar.wait_ge(S.go, 1)
     g.scalar.dma_start(T.y[:], cols(i)).then_inc(S.own, 16)
 
-    rid, pid, _ = topo.addr(peer(i ^ 2))
-    g.wait_ge(S.ldD, 16)
-    g.wait_ge(S.arr, 32)
-    g.remote_dma_fused(
-        [RemoteDMATransfer(dst_ids=[DstId(rid=rid, pnc=pid)], dma_engine_mask=ALL16, remote_sem=S.farr,
-                           srcs=[T.xs[2], T.land[0], T.land[1]], dsts=[T.fl[:]], alu_op=1)],
-        local_sem=S.fsent)
+    g.wait_ge(S.arr, 16)
+    fold([T.xs[4], T.land[0], T.land[1]], peer(i ^ 2), 0)
 
     g.wait_ge(S.own, 16)
-    g.wait_ge(S.farr, 16)
+    g.wait_ge(S.farr, 32)
     g.dma_start(T.y[:], T.fl[:], accum_op=AluOpType.add, max_dma_last_dim=4096).then_inc(S.done, 16)
-    g.wait_ge(S.sent, 32)
+    g.wait_ge(S.sent, 48)
     g.wait_ge(S.fsent, 16)
     g.wait_ge(S.done, 16)

@@ -9,7 +9,7 @@ SCRATCH = {
     "land": ("dram", [3, 128, H], "bfloat16"),
     "fl": ("dram", [2, 128, H], "bfloat16"),
 }
-SEMAPHORES = ["ldA", "ldB", "ldD", "own", "go", "sent", "arr", "fsent", "farr", "done"]
+SEMAPHORES = ["ldA", "ldB", "ldD", "ldK", "own", "go", "sent", "arr", "fsent", "farr", "done"]
 
 ALL16 = 0xFFFF
 LO8 = 0x00FF
@@ -49,7 +49,9 @@ def rank_program(g, core, T, topo):
 
     g.sync.dma_start(T.xs[0:2], cols(i ^ 1)).then_inc(S.ldA, 16)
     g.scalar.dma_start(T.xs[2:4], cols(i ^ 3)).then_inc(S.ldB, 16)
-    g.sync.dma_start(T.xs[4:6], cols(i ^ 2)).then_inc(S.ldD, 16)
+    d = (i ^ 2) * B
+    g.sync.dma_start(T.xs[5], T.x[64:128, d:d + B]).then_inc(S.ldD, 16)
+    g.scalar.dma_start(T.xs[4], T.x[0:64, d:d + B]).then_inc(S.ldK, 16)
 
     def send(slot, k, mslot):
         g.remote_dma_fused(
@@ -71,6 +73,7 @@ def rank_program(g, core, T, topo):
     g.scalar.wait_ge(S.go, 1)
     g.scalar.dma_start(T.y[:], cols(i)).then_inc(S.own, 16)
 
+    g.wait_ge(S.ldK, 16)
     g.wait_ge(S.arr, 16)
     fold([T.xs[4], T.land[0], T.land[1]], peer(i ^ 2), 0)
 

from concourse.bass import DstId, RemoteDMATransfer
from concourse.mybir import AluOpType

B = 512
H = 256

SCRATCH = {
    "xs": ("dram", [6, 128, H], "bfloat16"),
    "land": ("dram", [3, 128, H], "bfloat16"),
    "fl": ("dram", [2, 128, H], "bfloat16"),
}
SEMAPHORES = ["ldA", "ldB", "ldD", "ldK", "own", "go", "sent", "arr", "fsent", "farr", "done"]

ALL16 = 0xFFFF
LO8 = 0x00FF
HI8 = 0xFF00


def rank_program(g, core, T, topo):
    S = T.sem

    def dst(c):
        rid, pid, _ = topo.addr(c)
        return DstId(rid=rid, pnc=pid)

    def fold(srcs, owner, h):
        g.remote_dma_fused(
            [RemoteDMATransfer(dst_ids=[dst(owner)], dma_engine_mask=ALL16, remote_sem=S.farr,
                               srcs=srcs, dsts=[T.fl[h]], alu_op=1)],
            local_sem=S.fsent)

    rank = T.rank_of(core)
    if rank is None:
        if core + 2 >= 112 or topo.chip(core + 2) != topo.chip(core) or T.rank_of(core + 2) is None:
            return
        g.wait_ge(S.arr, 32)
        fold([T.land[0], T.land[1], T.land[2]], core + 2, 1)
        g.wait_ge(S.fsent, 16)
        return

    grp = [gr for gr in T.tables["GROUPS"] if rank in gr][0]
    i = grp.index(rank)

    def peer(k):
        return T.cores[grp[k]]

    def cols(b):
        return T.x[:, b * B:(b + 1) * B]

    g.sync.dma_start(T.xs[0:2], cols(i ^ 1)).then_inc(S.ldA, 16)
    g.scalar.dma_start(T.xs[2:4], cols(i ^ 3)).then_inc(S.ldB, 16)
    d = (i ^ 2) * B
    g.sync.dma_start(T.xs[5], T.x[64:128, d:d + B]).then_inc(S.ldD, 16)
    g.scalar.dma_start(T.xs[4], T.x[0:64, d:d + B]).then_inc(S.ldK, 16)

    def send(slot, k, mslot):
        g.remote_dma_fused(
            [RemoteDMATransfer(dst_ids=[dst(peer(i ^ k ^ 2))], dma_engine_mask=LO8, remote_sem=S.arr,
                               src=T.xs[slot], dst=T.land[mslot]),
             RemoteDMATransfer(dst_ids=[dst(peer(i ^ k) - 2)], dma_engine_mask=HI8, remote_sem=S.arr,
                               src=T.xs[slot + 1], dst=T.land[k - 1])],
            local_sem=S.sent)

    g.wait_ge(S.ldA, 16)
    send(0, 1, 1)
    g.wait_ge(S.ldB, 16)
    send(2, 3, 0)
    g.wait_ge(S.ldD, 16)
    rid, pid, _ = topo.addr(peer(i ^ 2) - 2)
    g.remote_dma(T.land[1], T.xs[5], S.arr, S.sent, pid, rid, ALL16)
    g.sem_inc(S.go, 1)

    g.scalar.wait_ge(S.go, 1)
    g.scalar.dma_start(T.y[:], cols(i)).then_inc(S.own, 16)

    g.wait_ge(S.ldK, 16)
    g.wait_ge(S.arr, 16)
    fold([T.xs[4], T.land[0], T.land[1]], peer(i ^ 2), 0)

    g.wait_ge(S.own, 16)
    g.wait_ge(S.farr, 32)
    g.dma_start(T.y[:], T.fl[:], accum_op=AluOpType.add, max_dma_last_dim=4096).then_inc(S.done, 16)
    g.wait_ge(S.sent, 48)
    g.wait_ge(S.fsent, 16)
    g.wait_ge(S.done, 16)
